import numpy as np
import ml_dtypes


def mxq(x, axis, fmt="e4m3"):
    dtype, down = {"e4m3": (ml_dtypes.float8_e4m3fn, 7), "e5m2": (ml_dtypes.float8_e5m2, 14)}[fmt]
    v = np.moveaxis(np.asarray(x, np.float32).astype(ml_dtypes.bfloat16).astype(np.float64), axis, -1)
    blocks = v.reshape(v.shape[:-1] + (-1, 32))
    amax = np.abs(blocks).max(-1, keepdims=True)
    byte = np.maximum(np.where(amax > 0, np.frexp(amax)[1] - 1 + 127, 0) - down, 1)
    scale = np.exp2(byte - 127.0)
    codes = (blocks / scale).astype(np.float32).astype(dtype).astype(np.float64)
    return np.moveaxis((codes * scale).reshape(v.shape), -1, axis)


WIDE = False


def mx_kscale(k):
    if not WIDE:
        return np.ones(k)
    levels = np.array([10, -10, 5, -5, 0])
    if k % 512:
        return np.exp2(np.random.permutation(np.resize(levels, k // 32))).repeat(32)
    a = np.empty((k // 512, 16))
    for p in range(k // 512):
        a[p, :8] = np.random.permutation(np.resize(levels, 8))
        for g in range(8):
            far = levels[np.abs(levels - a[p, g]) >= 10]
            a[p, g + 8] = far[np.random.randint(len(far))]
    return np.exp2(a.ravel()).repeat(32)


def f64(x):
    return np.asarray(x).astype(np.float64)


def striped(idx):
    return np.tile(idx.reshape(-1, 16).T, (8, 1)).astype(np.uint16)


def unstriped(offs):
    return offs[:16].T.reshape(-1).astype(np.int64)


def pack_weight(w):
    k, n = w.shape
    w = f64(np.asarray(w, np.float32).astype(ml_dtypes.bfloat16)).reshape(k // 32, 32, n)
    amax = np.abs(w).max(1)
    byte = np.clip(np.where(amax > 0, np.frexp(amax)[1] - 1 + 127 - 7, 1), 1, 254)
    scaled = (w * np.exp2(127.0 - byte)[:, None, :]).reshape(k, n).astype(np.float32)
    words = np.ascontiguousarray(scaled.reshape(k // 512, 128, 4, n).transpose(0, 1, 3, 2)).astype(ml_dtypes.float8_e4m3fn).view(np.uint8)
    return words, np.ascontiguousarray(byte.astype(np.uint8).reshape(k // 512, 16, n))


def unpack_weight(words, scales):
    g, p, n, _ = words.shape
    vals = np.ascontiguousarray(words).view(ml_dtypes.float8_e4m3fn).astype(np.float64) * np.repeat(np.exp2(scales.astype(np.float64) - 127.0), 8, axis=1)[..., None]
    return vals.transpose(0, 1, 3, 2).reshape(g * 512, n)


def gelu(v):
    return 0.5 * v * (1.0 + np.tanh(np.sqrt(2.0 / np.pi) * (v + 0.044715 * v**3)))


K, T, S, V, H, N = 512, 4096, 1536, 384, 512, 128


def setup_inputs():
    n = np.random.standard_normal
    s = mx_kscale(K)[:, None]
    u = mx_kscale(H)
    packed_xT = pack_weight(n((K, T)) * s)
    packed_w2 = pack_weight(n((H, N)) / np.sqrt(2 * H) / u[:, None])
    packed_w3 = pack_weight(n((H, N)) / np.sqrt(2 * H) / u[:, None])
    return {
        "x_words": packed_xT[0],
        "x_scales": packed_xT[1],
        "w1": (n((K, H)) / np.sqrt(K) / s * u).astype(np.float32),
        "w2_words": packed_w2[0],
        "w2_scales": packed_w2[1],
        "w3_words": packed_w3[0],
        "w3_scales": packed_w3[1],
        "offs": striped(np.random.permutation(T)[:S]),
    }


def reference(x_words, x_scales, w1, w2_words, w2_scales, w3_words, w3_scales, offs):
    xq = unpack_weight(x_words, x_scales)[:, unstriped(offs)]
    h = gelu(mxq(f64(w1), 0, "e4m3").T @ xq)
    mean = (h[:, :V] + h[:, V:2 * V] + h[:, 2 * V:3 * V] + h[:, 3 * V:4 * V]) / 4
    dev = np.sqrt(((h[:, :V] - mean) ** 2 + (h[:, V:2 * V] - mean) ** 2 + (h[:, 2 * V:3 * V] - mean) ** 2 + (h[:, 3 * V:4 * V] - mean) ** 2) / 4)
    return unpack_weight(w2_words, w2_scales).T @ mxq(mean, 0, "e4m3") + unpack_weight(w3_words, w3_scales).T @ mxq(dev, 0, "e4m3")

@@ -1,0 +1,205 @@
+import math
+from contextlib import ExitStack
+
+import concourse.mybir as mybir
+from concourse.masks import make_identity
+
+K, T, S, V, H, N = 512, 4096, 1536, 384, 512, 128
+D = 4
+P = 128
+PACK = 4
+BLOCKS = V // P
+GATHER = 512
+FLOPS = 2 * K * H * S + 2 * 2 * H * N * V
+
+F32 = mybir.dt.float32
+BF16 = mybir.dt.bfloat16
+I32 = mybir.dt.int32
+U32 = mybir.dt.uint32
+U16 = mybir.dt.uint16
+U8 = mybir.dt.uint8
+FP8X4 = mybir.dt.float8_e4m3fn_x4
+ACT = mybir.ActivationFunctionType
+ALU = mybir.AluOpType
+
+
+def load_scale_rows(nc, plane, rows):
+    for q in range(4):
+        nc.sync.dma_start(out=plane[32 * q : 32 * q + 4, :].bitcast(I32), in_=rows[4 * q : 4 * q + 4, :].bitcast(I32))
+
+
+def tile_picked_statpool_gelu_p_kernel(
+    tc, x_words, x_scales, w1, w2_words, w2_scales, w3_words, w3_scales, offs, out
+):
+    nc = tc.nc
+    with ExitStack() as ctx:
+        keep = ctx.enter_context(tc.tile_pool(name="keep", bufs=1))
+        psum = ctx.enter_context(tc.psum_pool(name="psum", bufs=1))
+
+        offsets = keep.tile([P, S // 16], U16, name="offsets")
+        nc.sync.dma_start(offsets[:], offs)
+
+        x_scale_table = keep.tile([P, T], U8, name="x_scale_table", align_bytes=64)
+        nc.vector.memset(x_scale_table[:].bitcast(I32), 0)
+        w23_scales = keep.tile([P, 2 * N], U8, name="w23_scales", align_bytes=64)
+        nc.vector.memset(w23_scales[:].bitcast(I32), 0)
+
+        w1_raw = keep.tile([P, PACK, H], F32, name="w1_raw")
+        nc.sync.dma_start(out=w1_raw[:], in_=w1.rearrange("(p j) c -> p j c", j=PACK))
+        load_scale_rows(nc, x_scale_table, x_scales[0])
+
+        x_word_table = keep.tile([P, T], U32, name="x_word_table", align_bytes=64)
+        x_flat = x_words[0].rearrange("p n t -> p (n t)").bitcast(I32)
+        for half in range(2):
+            cols = slice(half * T // 2, (half + 1) * T // 2)
+            nc.sync.dma_start(out=x_word_table[:, cols].bitcast(I32), in_=x_flat[:, cols])
+
+        w2_codes = keep.tile([P, N], U32, name="w2_codes", align_bytes=64)
+        w3_codes = keep.tile([P, N], U32, name="w3_codes", align_bytes=64)
+        nc.sync.dma_start(out=w2_codes[:].bitcast(I32), in_=w2_words[0].rearrange("p n t -> p (n t)").bitcast(I32))
+        nc.sync.dma_start(out=w3_codes[:].bitcast(I32), in_=w3_words[0].rearrange("p n t -> p (n t)").bitcast(I32))
+        load_scale_rows(nc, w23_scales[:, 0:N], w2_scales[0])
+        load_scale_rows(nc, w23_scales[:, N : 2 * N], w3_scales[0])
+
+        ident = keep.tile([P, P], F32, name="ident")
+        make_identity(nc, ident[:])
+
+        x_scales_picked = keep.tile([P, S], U8, name="x_scales_picked", align_bytes=64)
+        nc.vector.tensor_copy(x_scales_picked[:], x_scale_table[:].indirect(offsets[:]))
+
+        w1_grouped = keep.tile([P, PACK * H], BF16, name="w1_grouped", align_bytes=64)
+        nc.vector.tensor_copy(
+            out=w1_grouped[:].rearrange("p (t m j) -> p m t j", t=PACK, j=PACK),
+            in_=w1_raw[:].rearrange("p j (m t) -> p m t j", t=PACK),
+        )
+        w1_codes = keep.tile([P, H], U32, name="w1_codes", align_bytes=64)
+        w1_scales = keep.tile([P, H], U8, name="w1_scales", align_bytes=64)
+        nc.vector.quantize_mx(out=w1_codes[:].bitcast(FP8X4), scales=w1_scales[:], in_=w1_grouped[:])
+
+        x_words_picked = []
+        for g in range(S // GATHER):
+            picked = keep.tile([P, GATHER], U32, name="x_words_picked%d" % g, align_bytes=64)
+            nc.vector.tensor_copy(
+                picked[:], x_word_table[:].indirect(offsets[:, g * GATHER // 16 : (g + 1) * GATHER // 16])
+            )
+            x_words_picked.append(picked)
+
+        def wide(name):
+            return [keep.tile([P, H], F32, name="%s%d" % (name, b)) for b in range(BLOCKS)]
+
+        def bank_tile():
+            return psum.tile([P, PACK, P], F32, name="bank", tag="bank", bufs=8)
+
+        h = [wide("h%d_" % d) for d in range(D)]
+
+        def picked_block(d, b):
+            first = d * V + b * P
+            g, at = divmod(first, GATHER)
+            return x_words_picked[g][:, at : at + P].bitcast(FP8X4), x_scales_picked[:, first : first + P]
+
+        def hidden_by_segment(d, b):
+            words, scales = picked_block(d, b)
+            bank = bank_tile()
+            flat = bank[:].rearrange("p t m -> p (t m)")
+            nc.tensor.matmul_mx(
+                out=flat, lhsT=words, lhsT_scale=scales, rhs=w1_codes[:].bitcast(FP8X4), rhs_scale=w1_scales[:],
+                start=True, stop=True,
+            )
+            nc.scalar.activation(out=h[d][b][:], in_=flat, func=ACT.Gelu_apprx_tanh)
+
+        def hidden_by_channel(d, b):
+            words, scales = picked_block(d, b)
+            bank = bank_tile()
+            for t in range(PACK):
+                cols = slice(t * P, (t + 1) * P)
+                nc.tensor.matmul_mx(
+                    out=bank[:, t, :], lhsT=w1_codes[:, cols].bitcast(FP8X4), lhsT_scale=w1_scales[:, cols],
+                    rhs=words, rhs_scale=scales, start=True, stop=True,
+                )
+            nc.scalar.activation(out=h[d][b][:], in_=bank[:].rearrange("p t v -> p (t v)"), func=ACT.Gelu_apprx_tanh)
+
+        def add_transposed(bank, term, first, last):
+            for t in range(PACK):
+                nc.tensor.matmul(
+                    bank[:, t, :],
+                    lhsT=term[:, t * P : (t + 1) * P],
+                    rhs=ident[:],
+                    start=(first and t == 0),
+                    stop=(last and t == PACK - 1),
+                    is_transpose=True,
+                )
+
+        for b in range(BLOCKS):
+            hidden_by_segment(0, b)
+            hidden_by_segment(1, b)
+        for b in range(BLOCKS):
+            hidden_by_segment(2, b)
+        for b in range(BLOCKS):
+            hidden_by_channel(3, b)
+
+        sum2, z1, z2, z3, q1, q2, q3 = [wide(name) for name in ("sum2", "z1", "z2", "z3", "q1", "q2", "q3")]
+        total_bf = [keep.tile([P, P, PACK], BF16, name="total_bf%d" % b, align_bytes=64) for b in range(BLOCKS)]
+        dev_bf = [keep.tile([P, P, PACK], BF16, name="dev_bf%d" % b, align_bytes=64) for b in range(BLOCKS)]
+
+        for b in range(BLOCKS):
+            nc.vector.tensor_tensor(sum2[b][:], h[0][b][:], h[1][b][:], ALU.add)
+            nc.vector.tensor_tensor(z1[b][:], h[0][b][:], h[1][b][:], ALU.subtract)
+        sum3 = []
+        for b in range(BLOCKS):
+            nc.vector.scalar_tensor_tensor(z2[b][:], h[2][b][:], 2.0, sum2[b][:], ALU.mult, ALU.subtract)
+            sum3.append(bank_tile())
+            add_transposed(sum3[b], sum2[b], True, False)
+            add_transposed(sum3[b], h[2][b], False, True)
+        var = []
+        for b in range(BLOCKS):
+            nc.scalar.activation(out=q1[b][:], in_=z1[b][:], func=ACT.Square, scale=math.sqrt(2.0))
+            var.append(bank_tile())
+            add_transposed(var[b], q1[b], True, False)
+        for b in range(BLOCKS):
+            nc.vector.scalar_tensor_tensor(
+                z3[b][:], h[3][b][:], 3.0, sum3[b][:].rearrange("p t v -> p (t v)"), ALU.mult, ALU.subtract
+            )
+            turned = bank_tile()
+            add_transposed(turned, z3[b], True, True)
+            nc.scalar.activation(
+                out=q3[b][:], in_=turned[:].rearrange("p t m -> p (t m)"), func=ACT.Square, scale=math.sqrt(1.0 / 3.0)
+            )
+            add_transposed(var[b], q3[b], False, False)
+        for b in range(BLOCKS):
+            nc.vector.scalar_tensor_tensor(q2[b][:], z2[b][:], 2.0 / 3.0, z2[b][:], ALU.mult, ALU.mult)
+            add_transposed(var[b], q2[b], False, True)
+        for b in range(BLOCKS):
+            nc.vector.tensor_tensor(
+                total_bf[b][:],
+                sum3[b][:].rearrange("p t v -> p v t"),
+                h[3][b][:].rearrange("p (t v) -> p v t", t=PACK),
+                ALU.add,
+            )
+
+        def quantized(name, b, values):
+            codes = keep.tile([P, P], U32, name="%s_codes%d" % (name, b), align_bytes=64)
+            scales = keep.tile([P, P], U8, name="%s_scales%d" % (name, b), align_bytes=64)
+            nc.vector.quantize_mx(
+                out=codes[:].bitcast(FP8X4), scales=scales[:], in_=values[:].rearrange("p v t -> p (v t)")
+            )
+            return codes, scales
+
+        totals = [quantized("total", b, total_bf[b]) for b in range(BLOCKS)]
+        for b in range(BLOCKS):
+            nc.scalar.activation(out=dev_bf[b][:], in_=var[b][:].rearrange("p t v -> p v t"), func=ACT.Sqrt)
+        for b in range(BLOCKS):
+            passes = [(w2_codes, w23_scales[:, 0:N], totals[b]), (w3_codes, w23_scales[:, N : 2 * N], quantized("dev", b, dev_bf[b]))]
+            bank = bank_tile()
+            for u, (codes, scales, moving) in enumerate(passes):
+                nc.tensor.matmul_mx(
+                    out=bank[:, 0, :],
+                    lhsT=codes[:].bitcast(FP8X4),
+                    lhsT_scale=scales,
+                    rhs=moving[0][:].bitcast(FP8X4),
+                    rhs_scale=moving[1][:],
+                    start=(u == 0),
+                    stop=(u == 1),
+                )
+            result = keep.tile([P, P], F32, name="result%d" % b)
+            nc.vector.tensor_scalar(result[:], bank[:, 0, :], 1.0 / D, None, ALU.mult)
+            nc.sync.dma_start(out=out[:, b * P : (b + 1) * P], in_=result[:])

@@ -44,9 +44,11 @@ def tile_picked_statpool_gelu_p_kernel(
         w23_scales = keep.tile([P, 2 * N], U8, name="w23_scales", align_bytes=64)
         nc.vector.memset(w23_scales[:].bitcast(I32), 0)
 
-        w1_raw = keep.tile([P, PACK, H], F32, name="w1_raw")
-        nc.sync.dma_start(out=w1_raw[:], in_=w1.rearrange("(p j) c -> p j c", j=PACK))
+        w1_rows = w1.rearrange("(p j) c -> p j c", j=PACK)
+        w1_raw = [keep.tile([P, PACK, H // 2], F32, name="w1_raw%d" % half) for half in range(2)]
+        nc.sync.dma_start(out=w1_raw[0][:], in_=w1_rows[:, :, 0 : H // 2])
         load_scale_rows(nc, x_scale_table, x_scales[0])
+        nc.sync.dma_start(out=w1_raw[1][:], in_=w1_rows[:, :, H // 2 : H])
 
         x_word_table = keep.tile([P, T], U32, name="x_word_table", align_bytes=64)
         x_flat = x_words[0].rearrange("p n t -> p (n t)").bitcast(I32)
@@ -68,10 +70,11 @@ def tile_picked_statpool_gelu_p_kernel(
         nc.vector.tensor_copy(x_scales_picked[:], x_scale_table[:].indirect(offsets[:]))
 
         w1_grouped = keep.tile([P, PACK * H], BF16, name="w1_grouped", align_bytes=64)
-        nc.vector.tensor_copy(
-            out=w1_grouped[:].rearrange("p (t m j) -> p m t j", t=PACK, j=PACK),
-            in_=w1_raw[:].rearrange("p j (m t) -> p m t j", t=PACK),
-        )
+        for half in range(2):
+            nc.scalar.copy(
+                out=w1_grouped[:].rearrange("p (t m j) -> p m t j", t=PACK, j=PACK)[:, half * P // 2 : (half + 1) * P // 2],
+                in_=w1_raw[half][:].rearrange("p j (m t) -> p m t j", t=PACK),
+            )
         w1_codes = keep.tile([P, H], U32, name="w1_codes", align_bytes=64)
         w1_scales = keep.tile([P, H], U8, name="w1_scales", align_bytes=64)
         nc.vector.quantize_mx(out=w1_codes[:].bitcast(FP8X4), scales=w1_scales[:], in_=w1_grouped[:])
@@ -87,9 +90,10 @@ def tile_picked_statpool_gelu_p_kernel(
         def wide(name):
             return [keep.tile([P, H], F32, name="%s%d" % (name, b)) for b in range(BLOCKS)]
 
-        def bank_tile():
-            return psum.tile([P, PACK, P], F32, name="bank", tag="bank", bufs=8)
+        def bank_tile(index):
+            return psum.tile([P, PACK, P], F32, name="bank%d" % index, tag="bank%d" % index)
 
+        product_banks = (0, 1, 5, 6, 7)
         h = [wide("h%d_" % d) for d in range(D)]
 
         def picked_block(d, b):
@@ -97,26 +101,32 @@ def tile_picked_statpool_gelu_p_kernel(
             g, at = divmod(first, GATHER)
             return x_words_picked[g][:, at : at + P].bitcast(FP8X4), x_scales_picked[:, first : first + P]
 
-        def hidden_by_segment(d, b):
+        def flat(bank):
+            return bank[:].rearrange("p t c -> p (t c)")
+
+        def woven(bank):
+            return bank[:].rearrange("p t v -> p v t")
+
+        def by_word(tile):
+            return tile[:].rearrange("p (v t) -> p v t", t=PACK)
+
+        def hidden_by_segment(d, b, bank):
             words, scales = picked_block(d, b)
-            bank = bank_tile()
-            flat = bank[:].rearrange("p t m -> p (t m)")
             nc.tensor.matmul_mx(
-                out=flat, lhsT=words, lhsT_scale=scales, rhs=w1_codes[:].bitcast(FP8X4), rhs_scale=w1_scales[:],
+                out=flat(bank), lhsT=words, lhsT_scale=scales, rhs=w1_codes[:].bitcast(FP8X4), rhs_scale=w1_scales[:],
                 start=True, stop=True,
             )
-            nc.scalar.activation(out=h[d][b][:], in_=flat, func=ACT.Gelu_apprx_tanh)
+            nc.scalar.activation(out=h[d][b][:], in_=flat(bank), func=ACT.Gelu_apprx_tanh)
 
-        def hidden_by_channel(d, b):
+        def hidden_by_channel(d, b, bank):
             words, scales = picked_block(d, b)
-            bank = bank_tile()
             for t in range(PACK):
                 cols = slice(t * P, (t + 1) * P)
                 nc.tensor.matmul_mx(
                     out=bank[:, t, :], lhsT=w1_codes[:, cols].bitcast(FP8X4), lhsT_scale=w1_scales[:, cols],
                     rhs=words, rhs_scale=scales, start=True, stop=True,
                 )
-            nc.scalar.activation(out=h[d][b][:], in_=bank[:].rearrange("p t v -> p (t v)"), func=ACT.Gelu_apprx_tanh)
+            nc.scalar.activation(out=by_word(h[d][b]), in_=woven(bank), func=ACT.Gelu_apprx_tanh)
 
         def add_transposed(bank, term, first, last):
             for t in range(PACK):
@@ -129,17 +139,23 @@ def tile_picked_statpool_gelu_p_kernel(
                     is_transpose=True,
                 )
 
-        for b in range(BLOCKS):
-            hidden_by_segment(0, b)
-            hidden_by_segment(1, b)
-        for b in range(BLOCKS):
-            hidden_by_segment(2, b)
-        for b in range(BLOCKS):
-            hidden_by_channel(3, b)
+        order = [(d, b) for b in range(BLOCKS) for d in (0, 1)] + [(d, b) for d in (2, 3) for b in range(BLOCKS)]
+        for step, (d, b) in enumerate(order):
+            bank = bank_tile(product_banks[step % len(product_banks)])
+            if d == D - 1:
+                hidden_by_channel(d, b, bank)
+            else:
+                hidden_by_segment(d, b, bank)
 
-        sum2, z1, z2, z3, q1, q2, q3 = [wide(name) for name in ("sum2", "z1", "z2", "z3", "q1", "q2", "q3")]
-        total_bf = [keep.tile([P, P, PACK], BF16, name="total_bf%d" % b, align_bytes=64) for b in range(BLOCKS)]
-        dev_bf = [keep.tile([P, P, PACK], BF16, name="dev_bf%d" % b, align_bytes=64) for b in range(BLOCKS)]
+        sum2, z1, z2, z3, q1, q2, q3, var = [wide(name) for name in ("sum2", "z1", "z2", "z3", "q1", "q2", "q3", "var")]
+        total_bf = [keep.tile([P, H], BF16, name="total_bf%d" % b, align_bytes=64) for b in range(BLOCKS)]
+        dev_bf = [keep.tile([P, H], BF16, name="dev_bf%d" % b, align_bytes=64) for b in range(BLOCKS)]
+
+        def square(engine, q, z, weight):
+            if engine == "S":
+                nc.scalar.activation(out=q[:], in_=z[:], func=ACT.Square, scale=math.sqrt(weight))
+            else:
+                nc.vector.scalar_tensor_tensor(q[:], z[:], weight, z[:], ALU.mult, ALU.mult)
 
         for b in range(BLOCKS):
             nc.vector.tensor_tensor(sum2[b][:], h[0][b][:], h[1][b][:], ALU.add)
@@ -147,49 +163,38 @@ def tile_picked_statpool_gelu_p_kernel(
         sum3 = []
         for b in range(BLOCKS):
             nc.vector.scalar_tensor_tensor(z2[b][:], h[2][b][:], 2.0, sum2[b][:], ALU.mult, ALU.subtract)
-            sum3.append(bank_tile())
-            add_transposed(sum3[b], sum2[b], True, False)
-            add_transposed(sum3[b], h[2][b], False, True)
-        var = []
+            sum3.append(bank_tile(2 + b))
+            add_transposed(sum3[b], h[2][b], True, False)
+            add_transposed(sum3[b], sum2[b], False, True)
+        q12 = []
         for b in range(BLOCKS):
-            nc.scalar.activation(out=q1[b][:], in_=z1[b][:], func=ACT.Square, scale=math.sqrt(2.0))
-            var.append(bank_tile())
-            add_transposed(var[b], q1[b], True, False)
+            square("S", q1[b], z1[b], 2.0)
+            q12.append(bank_tile(5 + b))
+            add_transposed(q12[b], q1[b], True, False)
         for b in range(BLOCKS):
-            nc.vector.scalar_tensor_tensor(
-                z3[b][:], h[3][b][:], 3.0, sum3[b][:].rearrange("p t v -> p (t v)"), ALU.mult, ALU.subtract
-            )
-            turned = bank_tile()
-            add_transposed(turned, z3[b], True, True)
-            nc.scalar.activation(
-                out=q3[b][:], in_=turned[:].rearrange("p t m -> p (t m)"), func=ACT.Square, scale=math.sqrt(1.0 / 3.0)
-            )
-            add_transposed(var[b], q3[b], False, False)
+            nc.vector.scalar_tensor_tensor(by_word(z3[b]), by_word(h[3][b]), 3.0, woven(sum3[b]), ALU.mult, ALU.subtract)
+            square("SVV"[b], q3[b], z3[b], 1.0 / 3.0)
         for b in range(BLOCKS):
-            nc.vector.scalar_tensor_tensor(q2[b][:], z2[b][:], 2.0 / 3.0, z2[b][:], ALU.mult, ALU.mult)
-            add_transposed(var[b], q2[b], False, True)
+            square("S", q2[b], z2[b], 2.0 / 3.0)
+            add_transposed(q12[b], q2[b], False, True)
         for b in range(BLOCKS):
-            nc.vector.tensor_tensor(
-                total_bf[b][:],
-                sum3[b][:].rearrange("p t v -> p v t"),
-                h[3][b][:].rearrange("p (t v) -> p v t", t=PACK),
-                ALU.add,
-            )
+            nc.vector.tensor_tensor(by_word(var[b]), woven(q12[b]), by_word(q3[b]), ALU.add)
+        for b in range(BLOCKS):
+            nc.scalar.activation(out=dev_bf[b][:], in_=var[b][:], func=ACT.Sqrt)
 
         def quantized(name, b, values):
             codes = keep.tile([P, P], U32, name="%s_codes%d" % (name, b), align_bytes=64)
             scales = keep.tile([P, P], U8, name="%s_scales%d" % (name, b), align_bytes=64)
-            nc.vector.quantize_mx(
-                out=codes[:].bitcast(FP8X4), scales=scales[:], in_=values[:].rearrange("p v t -> p (v t)")
-            )
+            nc.vector.quantize_mx(out=codes[:].bitcast(FP8X4), scales=scales[:], in_=values[:])
             return codes, scales
 
-        totals = [quantized("total", b, total_bf[b]) for b in range(BLOCKS)]
         for b in range(BLOCKS):
-            nc.scalar.activation(out=dev_bf[b][:], in_=var[b][:].rearrange("p t v -> p v t"), func=ACT.Sqrt)
-        for b in range(BLOCKS):
-            passes = [(w2_codes, w23_scales[:, 0:N], totals[b]), (w3_codes, w23_scales[:, N : 2 * N], quantized("dev", b, dev_bf[b]))]
-            bank = bank_tile()
+            nc.vector.tensor_tensor(by_word(total_bf[b]), woven(sum3[b]), by_word(h[3][b]), ALU.add)
+            passes = [
+                (w2_codes, w23_scales[:, 0:N], quantized("total", b, total_bf[b])),
+                (w3_codes, w23_scales[:, N : 2 * N], quantized("dev", b, dev_bf[b])),
+            ]
+            bank = bank_tile(b % 2)
             for u, (codes, scales, moving) in enumerate(passes):
                 nc.tensor.matmul_mx(
                     out=bank[:, 0, :],
@@ -201,5 +206,5 @@ def tile_picked_statpool_gelu_p_kernel(
                     stop=(u == 1),
                 )
             result = keep.tile([P, P], F32, name="result%d" % b)
-            nc.vector.tensor_scalar(result[:], bank[:, 0, :], 1.0 / D, None, ALU.mult)
+            nc.scalar.activation(out=result[:], in_=bank[:, 0, :], func=ACT.Copy, scale=1.0 / D)
             nc.sync.dma_start(out=out[:, b * P : (b + 1) * P], in_=result[:])

@@ -24,8 +24,8 @@ ALU = mybir.AluOpType
 
 
 def load_scale_rows(nc, plane, rows):
-    for q in range(4):
-        nc.sync.dma_start(out=plane[32 * q : 32 * q + 4, :].bitcast(I32), in_=rows[4 * q : 4 * q + 4, :].bitcast(I32))
+    for r in range(4):
+        nc.sync.dma_start(out=plane[r:P:32, :].bitcast(I32), in_=rows[r:16:4, :].bitcast(I32))
 
 
 def tile_picked_statpool_gelu_p_kernel(
@@ -40,14 +40,13 @@ def tile_picked_statpool_gelu_p_kernel(
         nc.sync.dma_start(offsets[:], offs)
 
         x_scale_table = keep.tile([P, T], U8, name="x_scale_table", align_bytes=64)
-        nc.vector.memset(x_scale_table[:].bitcast(I32), 0)
-        w23_scales = keep.tile([P, 2 * N], U8, name="w23_scales", align_bytes=64)
-        nc.vector.memset(w23_scales[:].bitcast(I32), 0)
+        nc.gpsimd.memset(x_scale_table[:, 0 : T // 2].bitcast(I32), 0)
+        nc.vector.memset(x_scale_table[:, T // 2 : T].bitcast(I32), 0)
 
         w1_rows = w1.rearrange("(p j) c -> p j c", j=PACK)
-        w1_raw = [keep.tile([P, PACK, H // 2], F32, name="w1_raw%d" % half) for half in range(2)]
+        w1_raw = [keep.tile([P, PACK, H // 2], F32, name="w1_raw%d" % half, tag="w1_raw%d" % half, align_bytes=64) for half in range(2)]
         nc.sync.dma_start(out=w1_raw[0][:], in_=w1_rows[:, :, 0 : H // 2])
-        load_scale_rows(nc, x_scale_table, x_scales[0])
+        nc.sync.dma_start(out=x_scale_table[4:P:8, :].bitcast(I32), in_=x_scales[0].bitcast(I32))
         nc.sync.dma_start(out=w1_raw[1][:], in_=w1_rows[:, :, H // 2 : H])
 
         x_word_table = keep.tile([P, T], U32, name="x_word_table", align_bytes=64)
@@ -60,24 +59,32 @@ def tile_picked_statpool_gelu_p_kernel(
         w3_codes = keep.tile([P, N], U32, name="w3_codes", align_bytes=64)
         nc.sync.dma_start(out=w2_codes[:].bitcast(I32), in_=w2_words[0].rearrange("p n t -> p (n t)").bitcast(I32))
         nc.sync.dma_start(out=w3_codes[:].bitcast(I32), in_=w3_words[0].rearrange("p n t -> p (n t)").bitcast(I32))
-        load_scale_rows(nc, w23_scales[:, 0:N], w2_scales[0])
-        load_scale_rows(nc, w23_scales[:, N : 2 * N], w3_scales[0])
 
         ident = keep.tile([P, P], F32, name="ident")
         make_identity(nc, ident[:])
 
-        x_scales_picked = keep.tile([P, S], U8, name="x_scales_picked", align_bytes=64)
-        nc.vector.tensor_copy(x_scales_picked[:], x_scale_table[:].indirect(offsets[:]))
+        x_scales_spread = keep.tile([P, S], U8, name="x_scales_spread", align_bytes=64)
+        nc.vector.tensor_copy(x_scales_spread[:], x_scale_table[:].indirect(offsets[:]))
 
-        w1_grouped = keep.tile([P, PACK * H], BF16, name="w1_grouped", align_bytes=64)
+        w1_grouped = keep.tile([P, PACK * H], BF16, name="w1_grouped", tag="w1_grouped", align_bytes=64)
         for half in range(2):
             nc.scalar.copy(
                 out=w1_grouped[:].rearrange("p (t m j) -> p m t j", t=PACK, j=PACK)[:, half * P // 2 : (half + 1) * P // 2],
                 in_=w1_raw[half][:].rearrange("p j (m t) -> p m t j", t=PACK),
             )
+        x_scales_picked = keep.tile([P, S], U8, name="x_scales_picked", tag="w1_raw1", align_bytes=64)
+        nc.gpsimd.memset(x_scales_picked[:].bitcast(I32), 0)
+        for r in range(4):
+            nc.scalar.dma_start(
+                out=x_scales_picked[r:P:32, :].bitcast(I32), in_=x_scales_spread[8 * r + 4 : P : 32, :].bitcast(I32)
+            )
         w1_codes = keep.tile([P, H], U32, name="w1_codes", align_bytes=64)
         w1_scales = keep.tile([P, H], U8, name="w1_scales", align_bytes=64)
         nc.vector.quantize_mx(out=w1_codes[:].bitcast(FP8X4), scales=w1_scales[:], in_=w1_grouped[:])
+        w23_scales = keep.tile([P, 2 * N], U8, name="w23_scales", tag="w1_grouped", align_bytes=64)
+        nc.gpsimd.memset(w23_scales[:].bitcast(I32), 0)
+        load_scale_rows(nc, w23_scales[:, 0:N], w2_scales[0])
+        load_scale_rows(nc, w23_scales[:, N : 2 * N], w3_scales[0])
 
         x_words_picked = []
         for g in range(S // GATHER):

@@ -43,11 +43,11 @@ def tile_picked_statpool_gelu_p_kernel(
         nc.gpsimd.memset(x_scale_table[:, 0 : T // 2].bitcast(I32), 0)
         nc.vector.memset(x_scale_table[:, T // 2 : T].bitcast(I32), 0)
 
+        w1_raw = keep.tile([P, PACK, H], F32, name="w1_raw")
         w1_rows = w1.rearrange("(p j) c -> p j c", j=PACK)
-        w1_raw = [keep.tile([P, PACK, H // 2], F32, name="w1_raw%d" % half, tag="w1_raw%d" % half, align_bytes=64) for half in range(2)]
-        nc.sync.dma_start(out=w1_raw[0][:], in_=w1_rows[:, :, 0 : H // 2])
+        nc.sync.dma_start(out=w1_raw[:, 0:2, :], in_=w1_rows[:, 0:2, :])
         nc.sync.dma_start(out=x_scale_table[4:P:8, :].bitcast(I32), in_=x_scales[0].bitcast(I32))
-        nc.sync.dma_start(out=w1_raw[1][:], in_=w1_rows[:, :, H // 2 : H])
+        nc.sync.dma_start(out=w1_raw[:, 2:4, :], in_=w1_rows[:, 2:4, :])
 
         x_word_table = keep.tile([P, T], U32, name="x_word_table", align_bytes=64)
         x_flat = x_words[0].rearrange("p n t -> p (n t)").bitcast(I32)
@@ -67,12 +67,11 @@ def tile_picked_statpool_gelu_p_kernel(
         nc.vector.tensor_copy(x_scales_spread[:], x_scale_table[:].indirect(offsets[:]))
 
         w1_grouped = keep.tile([P, PACK * H], BF16, name="w1_grouped", tag="w1_grouped", align_bytes=64)
-        for half in range(2):
-            nc.scalar.copy(
-                out=w1_grouped[:].rearrange("p (t m j) -> p m t j", t=PACK, j=PACK)[:, half * P // 2 : (half + 1) * P // 2],
-                in_=w1_raw[half][:].rearrange("p j (m t) -> p m t j", t=PACK),
-            )
-        x_scales_picked = keep.tile([P, S], U8, name="x_scales_picked", tag="w1_raw1", align_bytes=64)
+        nc.vector.tensor_copy(
+            out=w1_grouped[:].rearrange("p (t m j) -> p m t j", t=PACK, j=PACK),
+            in_=w1_raw[:].rearrange("p j (m t) -> p m t j", t=PACK),
+        )
+        x_scales_picked = keep.tile([P, S], U8, name="x_scales_picked", align_bytes=64)
         nc.gpsimd.memset(x_scales_picked[:].bitcast(I32), 0)
         for r in range(4):
             nc.scalar.dma_start(
@@ -101,7 +100,8 @@ def tile_picked_statpool_gelu_p_kernel(
             return psum.tile([P, PACK, P], F32, name="bank%d" % index, tag="bank%d" % index)
 
         product_banks = (0, 1, 5, 6, 7)
-        h = [wide("h%d_" % d) for d in range(D)]
+        h_all = [keep.tile([P, BLOCKS, H], F32, name="h%d" % d) for d in range(D)]
+        h = [[h_all[d][:, b, :] for b in range(BLOCKS)] for d in range(D)]
 
         def picked_block(d, b):
             first = d * V + b * P
@@ -115,7 +115,7 @@ def tile_picked_statpool_gelu_p_kernel(
             return bank[:].rearrange("p t v -> p v t")
 
         def by_word(tile):
-            return tile[:].rearrange("p (v t) -> p v t", t=PACK)
+            return tile[:, :].rearrange("p (v t) -> p v t", t=PACK)
 
         def hidden_by_segment(d, b, bank):
             words, scales = picked_block(d, b)
@@ -123,7 +123,7 @@ def tile_picked_statpool_gelu_p_kernel(
                 out=flat(bank), lhsT=words, lhsT_scale=scales, rhs=w1_codes[:].bitcast(FP8X4), rhs_scale=w1_scales[:],
                 start=True, stop=True,
             )
-            nc.scalar.activation(out=h[d][b][:], in_=flat(bank), func=ACT.Gelu_apprx_tanh)
+            nc.scalar.activation(out=h[d][b], in_=flat(bank), func=ACT.Gelu_apprx_tanh)
 
         def hidden_by_channel(d, b, bank):
             words, scales = picked_block(d, b)
@@ -154,61 +154,69 @@ def tile_picked_statpool_gelu_p_kernel(
             else:
                 hidden_by_segment(d, b, bank)
 
-        sum2, z1, z2, z3, q1, q2, q3, var = [wide(name) for name in ("sum2", "z1", "z2", "z3", "q1", "q2", "q3", "var")]
-        total_bf = [keep.tile([P, H], BF16, name="total_bf%d" % b, align_bytes=64) for b in range(BLOCKS)]
-        dev_bf = [keep.tile([P, H], BF16, name="dev_bf%d" % b, align_bytes=64) for b in range(BLOCKS)]
+        z1, z3, q1, q2, q3, var = [wide(name) for name in ("z1", "z3", "q1", "q2", "q3", "var")]
+        sum2 = keep.tile([P, BLOCKS, H], F32, name="sum2")
+        z2 = keep.tile([P, BLOCKS, H], F32, name="z2")
+        stats_bf = keep.tile([P, 2 * BLOCKS, H], BF16, name="stats_bf", align_bytes=64)
+        stats_codes = keep.tile([P, 2 * BLOCKS, P], U32, name="stats_codes", align_bytes=64)
+        stats_scales = keep.tile([P, 2 * BLOCKS, P], U8, name="stats_scales", align_bytes=64)
 
-        def square(engine, q, z, weight):
-            if engine == "S":
-                nc.scalar.activation(out=q[:], in_=z[:], func=ACT.Square, scale=math.sqrt(weight))
-            else:
-                nc.vector.scalar_tensor_tensor(q[:], z[:], weight, z[:], ALU.mult, ALU.mult)
+        def square(q, z, weight):
+            nc.scalar.activation(out=q, in_=z, func=ACT.Square, scale=math.sqrt(weight))
 
         for b in range(BLOCKS):
-            nc.vector.tensor_tensor(sum2[b][:], h[0][b][:], h[1][b][:], ALU.add)
-            nc.vector.tensor_tensor(z1[b][:], h[0][b][:], h[1][b][:], ALU.subtract)
+            nc.vector.tensor_tensor(sum2[:, b, :], h[0][b], h[1][b], ALU.add)
+            nc.vector.tensor_tensor(z1[b][:], h[0][b], h[1][b], ALU.subtract)
+        for blocks in (slice(0, 1), slice(1, BLOCKS)):
+            nc.vector.scalar_tensor_tensor(
+                z2[:, blocks, :], h_all[2][:, blocks, :], 2.0, sum2[:, blocks, :], ALU.mult, ALU.subtract
+            )
         sum3 = []
         for b in range(BLOCKS):
-            nc.vector.scalar_tensor_tensor(z2[b][:], h[2][b][:], 2.0, sum2[b][:], ALU.mult, ALU.subtract)
             sum3.append(bank_tile(2 + b))
             add_transposed(sum3[b], h[2][b], True, False)
-            add_transposed(sum3[b], sum2[b], False, True)
+            add_transposed(sum3[b], sum2[:, b, :], False, True)
         q12 = []
         for b in range(BLOCKS):
-            square("S", q1[b], z1[b], 2.0)
+            square(q1[b][:], z1[b][:], 3.0)
             q12.append(bank_tile(5 + b))
             add_transposed(q12[b], q1[b], True, False)
         for b in range(BLOCKS):
             nc.vector.scalar_tensor_tensor(by_word(z3[b]), by_word(h[3][b]), 3.0, woven(sum3[b]), ALU.mult, ALU.subtract)
-            square("SVV"[b], q3[b], z3[b], 1.0 / 3.0)
         for b in range(BLOCKS):
-            square("S", q2[b], z2[b], 2.0 / 3.0)
+            if b == 0:
+                square(q2[b][:], z2[:, b, :], 1.0)
+            else:
+                nc.gpsimd.tensor_tensor(q2[b][:], z2[:, b, :], z2[:, b, :], ALU.mult)
             add_transposed(q12[b], q2[b], False, True)
         for b in range(BLOCKS):
-            nc.vector.tensor_tensor(by_word(var[b]), woven(q12[b]), by_word(q3[b]), ALU.add)
+            if b < BLOCKS - 1:
+                square(q3[b][:], z3[b][:], 1.0)
+            else:
+                nc.gpsimd.tensor_tensor(q3[b][:], z3[b][:], z3[b][:], ALU.mult)
         for b in range(BLOCKS):
-            nc.scalar.activation(out=dev_bf[b][:], in_=var[b][:], func=ACT.Sqrt)
-
-        def quantized(name, b, values):
-            codes = keep.tile([P, P], U32, name="%s_codes%d" % (name, b), align_bytes=64)
-            scales = keep.tile([P, P], U8, name="%s_scales%d" % (name, b), align_bytes=64)
-            nc.vector.quantize_mx(out=codes[:].bitcast(FP8X4), scales=scales[:], in_=values[:])
-            return codes, scales
+            nc.vector.tensor_tensor(by_word(stats_bf[:, b, :]), woven(sum3[b]), by_word(h[3][b]), ALU.add)
+        for b in range(BLOCKS):
+            nc.vector.scalar_tensor_tensor(by_word(var[b]), by_word(q3[b]), 0.5, woven(q12[b]), ALU.mult, ALU.add)
+        for b in range(BLOCKS):
+            nc.scalar.activation(out=stats_bf[:, BLOCKS + b, :], in_=var[b][:], func=ACT.Sqrt, scale=2.0 / 3.0)
+        for rows in (slice(0, BLOCKS + 1), slice(BLOCKS + 1, BLOCKS + 2), slice(BLOCKS + 2, 2 * BLOCKS)):
+            nc.vector.quantize_mx(
+                out=stats_codes[:, rows, :].rearrange("p r c -> p (r c)").bitcast(FP8X4),
+                scales=stats_scales[:, rows, :].rearrange("p r c -> p (r c)"),
+                in_=stats_bf[:, rows, :].rearrange("p r c -> p (r c)"),
+            )
 
         for b in range(BLOCKS):
-            nc.vector.tensor_tensor(by_word(total_bf[b]), woven(sum3[b]), by_word(h[3][b]), ALU.add)
-            passes = [
-                (w2_codes, w23_scales[:, 0:N], quantized("total", b, total_bf[b])),
-                (w3_codes, w23_scales[:, N : 2 * N], quantized("dev", b, dev_bf[b])),
-            ]
-            bank = bank_tile(b % 2)
-            for u, (codes, scales, moving) in enumerate(passes):
+            passes = [(w2_codes, w23_scales[:, 0:N], b), (w3_codes, w23_scales[:, N : 2 * N], BLOCKS + b)]
+            bank = bank_tile(b)
+            for u, (codes, scales, row) in enumerate(passes):
                 nc.tensor.matmul_mx(
                     out=bank[:, 0, :],
                     lhsT=codes[:].bitcast(FP8X4),
                     lhsT_scale=scales,
-                    rhs=moving[0][:].bitcast(FP8X4),
-                    rhs_scale=moving[1][:],
+                    rhs=stats_codes[:, row, :].bitcast(FP8X4),
+                    rhs_scale=stats_scales[:, row, :],
                     start=(u == 0),
                     stop=(u == 1),
                 )

import math
from contextlib import ExitStack

import concourse.mybir as mybir
from concourse.masks import make_identity

K, T, S, V, H, N = 512, 4096, 1536, 384, 512, 128
D = 4
P = 128
PACK = 4
BLOCKS = V // P
GATHER = 512
FLOPS = 2 * K * H * S + 2 * 2 * H * N * V

F32 = mybir.dt.float32
BF16 = mybir.dt.bfloat16
I32 = mybir.dt.int32
U32 = mybir.dt.uint32
U16 = mybir.dt.uint16
U8 = mybir.dt.uint8
FP8X4 = mybir.dt.float8_e4m3fn_x4
ACT = mybir.ActivationFunctionType
ALU = mybir.AluOpType


def load_scale_rows(nc, plane, rows):
    for r in range(4):
        nc.sync.dma_start(out=plane[r:P:32, :].bitcast(I32), in_=rows[r:16:4, :].bitcast(I32))


def tile_picked_statpool_gelu_p_kernel(
    tc, x_words, x_scales, w1, w2_words, w2_scales, w3_words, w3_scales, offs, out
):
    nc = tc.nc
    with ExitStack() as ctx:
        keep = ctx.enter_context(tc.tile_pool(name="keep", bufs=1))
        psum = ctx.enter_context(tc.psum_pool(name="psum", bufs=1))

        offsets = keep.tile([P, S // 16], U16, name="offsets")
        nc.sync.dma_start(offsets[:], offs)

        x_scale_table = keep.tile([P, T], U8, name="x_scale_table", align_bytes=64)
        nc.gpsimd.memset(x_scale_table[:, 0 : T // 2].bitcast(I32), 0)
        nc.vector.memset(x_scale_table[:, T // 2 : T].bitcast(I32), 0)

        w1_raw = keep.tile([P, PACK, H], F32, name="w1_raw")
        w1_rows = w1.rearrange("(p j) c -> p j c", j=PACK)
        nc.sync.dma_start(out=w1_raw[:, 0:2, :], in_=w1_rows[:, 0:2, :])
        nc.sync.dma_start(out=x_scale_table[4:P:8, :].bitcast(I32), in_=x_scales[0].bitcast(I32))
        nc.sync.dma_start(out=w1_raw[:, 2:4, :], in_=w1_rows[:, 2:4, :])

        x_word_table = keep.tile([P, T], U32, name="x_word_table", align_bytes=64)
        x_flat = x_words[0].rearrange("p n t -> p (n t)").bitcast(I32)
        for half in range(2):
            cols = slice(half * T // 2, (half + 1) * T // 2)
            nc.sync.dma_start(out=x_word_table[:, cols].bitcast(I32), in_=x_flat[:, cols])

        w2_codes = keep.tile([P, N], U32, name="w2_codes", align_bytes=64)
        w3_codes = keep.tile([P, N], U32, name="w3_codes", align_bytes=64)
        nc.sync.dma_start(out=w2_codes[:].bitcast(I32), in_=w2_words[0].rearrange("p n t -> p (n t)").bitcast(I32))
        nc.sync.dma_start(out=w3_codes[:].bitcast(I32), in_=w3_words[0].rearrange("p n t -> p (n t)").bitcast(I32))

        ident = keep.tile([P, P], F32, name="ident")
        make_identity(nc, ident[:])

        x_scales_spread = keep.tile([P, S], U8, name="x_scales_spread", align_bytes=64)
        nc.vector.tensor_copy(x_scales_spread[:], x_scale_table[:].indirect(offsets[:]))

        w1_grouped = keep.tile([P, PACK * H], BF16, name="w1_grouped", tag="w1_grouped", align_bytes=64)
        nc.vector.tensor_copy(
            out=w1_grouped[:].rearrange("p (t m j) -> p m t j", t=PACK, j=PACK),
            in_=w1_raw[:].rearrange("p j (m t) -> p m t j", t=PACK),
        )
        x_scales_picked = keep.tile([P, S], U8, name="x_scales_picked", align_bytes=64)
        nc.gpsimd.memset(x_scales_picked[:].bitcast(I32), 0)
        for r in range(4):
            nc.scalar.dma_start(
                out=x_scales_picked[r:P:32, :].bitcast(I32), in_=x_scales_spread[8 * r + 4 : P : 32, :].bitcast(I32)
            )
        w1_codes = keep.tile([P, H], U32, name="w1_codes", align_bytes=64)
        w1_scales = keep.tile([P, H], U8, name="w1_scales", align_bytes=64)
        nc.vector.quantize_mx(out=w1_codes[:].bitcast(FP8X4), scales=w1_scales[:], in_=w1_grouped[:])
        w23_scales = keep.tile([P, 2 * N], U8, name="w23_scales", tag="w1_grouped", align_bytes=64)
        nc.gpsimd.memset(w23_scales[:].bitcast(I32), 0)
        load_scale_rows(nc, w23_scales[:, 0:N], w2_scales[0])
        load_scale_rows(nc, w23_scales[:, N : 2 * N], w3_scales[0])

        x_words_picked = []
        for g in range(S // GATHER):
            picked = keep.tile([P, GATHER], U32, name="x_words_picked%d" % g, align_bytes=64)
            nc.vector.tensor_copy(
                picked[:], x_word_table[:].indirect(offsets[:, g * GATHER // 16 : (g + 1) * GATHER // 16])
            )
            x_words_picked.append(picked)

        def wide(name):
            return [keep.tile([P, H], F32, name="%s%d" % (name, b)) for b in range(BLOCKS)]

        def bank_tile(index):
            return psum.tile([P, PACK, P], F32, name="bank%d" % index, tag="bank%d" % index)

        product_banks = (0, 1, 5, 6, 7)
        h_all = [keep.tile([P, BLOCKS, H], F32, name="h%d" % d) for d in range(D)]
        h = [[h_all[d][:, b, :] for b in range(BLOCKS)] for d in range(D)]

        def picked_block(d, b):
            first = d * V + b * P
            g, at = divmod(first, GATHER)
            return x_words_picked[g][:, at : at + P].bitcast(FP8X4), x_scales_picked[:, first : first + P]

        def flat(bank):
            return bank[:].rearrange("p t c -> p (t c)")

        def woven(bank):
            return bank[:].rearrange("p t v -> p v t")

        def by_word(tile):
            return tile[:, :].rearrange("p (v t) -> p v t", t=PACK)

        def hidden_by_segment(d, b, bank):
            words, scales = picked_block(d, b)
            nc.tensor.matmul_mx(
                out=flat(bank), lhsT=words, lhsT_scale=scales, rhs=w1_codes[:].bitcast(FP8X4), rhs_scale=w1_scales[:],
                start=True, stop=True,
            )
            nc.scalar.activation(out=h[d][b], in_=flat(bank), func=ACT.Gelu_apprx_tanh)

        def hidden_by_channel(d, b, bank):
            words, scales = picked_block(d, b)
            for t in range(PACK):
                cols = slice(t * P, (t + 1) * P)
                nc.tensor.matmul_mx(
                    out=bank[:, t, :], lhsT=w1_codes[:, cols].bitcast(FP8X4), lhsT_scale=w1_scales[:, cols],
                    rhs=words, rhs_scale=scales, start=True, stop=True,
                )
            nc.scalar.activation(out=by_word(h[d][b]), in_=woven(bank), func=ACT.Gelu_apprx_tanh)

        def add_transposed(bank, term, first, last):
            for t in range(PACK):
                nc.tensor.matmul(
                    bank[:, t, :],
                    lhsT=term[:, t * P : (t + 1) * P],
                    rhs=ident[:],
                    start=(first and t == 0),
                    stop=(last and t == PACK - 1),
                    is_transpose=True,
                )

        order = [(d, b) for b in range(BLOCKS) for d in (0, 1)] + [(d, b) for d in (2, 3) for b in range(BLOCKS)]
        for step, (d, b) in enumerate(order):
            bank = bank_tile(product_banks[step % len(product_banks)])
            if d == D - 1:
                hidden_by_channel(d, b, bank)
            else:
                hidden_by_segment(d, b, bank)

        z1, z3, q1, q2, q3, var = [wide(name) for name in ("z1", "z3", "q1", "q2", "q3", "var")]
        sum2 = keep.tile([P, BLOCKS, H], F32, name="sum2")
        z2 = keep.tile([P, BLOCKS, H], F32, name="z2")
        stats_bf = keep.tile([P, 2 * BLOCKS, H], BF16, name="stats_bf", align_bytes=64)
        stats_codes = keep.tile([P, 2 * BLOCKS, P], U32, name="stats_codes", align_bytes=64)
        stats_scales = keep.tile([P, 2 * BLOCKS, P], U8, name="stats_scales", align_bytes=64)

        def square(q, z, weight):
            nc.scalar.activation(out=q, in_=z, func=ACT.Square, scale=math.sqrt(weight))

        for b in range(BLOCKS):
            nc.vector.tensor_tensor(sum2[:, b, :], h[0][b], h[1][b], ALU.add)
            nc.vector.tensor_tensor(z1[b][:], h[0][b], h[1][b], ALU.subtract)
        for blocks in (slice(0, 1), slice(1, BLOCKS)):
            nc.vector.scalar_tensor_tensor(
                z2[:, blocks, :], h_all[2][:, blocks, :], 2.0, sum2[:, blocks, :], ALU.mult, ALU.subtract
            )
        sum3 = []
        for b in range(BLOCKS):
            sum3.append(bank_tile(2 + b))
            add_transposed(sum3[b], h[2][b], True, False)
            add_transposed(sum3[b], sum2[:, b, :], False, True)
        q12 = []
        for b in range(BLOCKS):
            square(q1[b][:], z1[b][:], 3.0)
            q12.append(bank_tile(5 + b))
            add_transposed(q12[b], q1[b], True, False)
        for b in range(BLOCKS):
            nc.vector.scalar_tensor_tensor(by_word(z3[b]), by_word(h[3][b]), 3.0, woven(sum3[b]), ALU.mult, ALU.subtract)
        for b in range(BLOCKS):
            if b == 0:
                square(q2[b][:], z2[:, b, :], 1.0)
            else:
                nc.gpsimd.tensor_tensor(q2[b][:], z2[:, b, :], z2[:, b, :], ALU.mult)
            add_transposed(q12[b], q2[b], False, True)
        for b in range(BLOCKS):
            if b < BLOCKS - 1:
                square(q3[b][:], z3[b][:], 1.0)
            else:
                nc.gpsimd.tensor_tensor(q3[b][:], z3[b][:], z3[b][:], ALU.mult)
        for b in range(BLOCKS):
            nc.vector.tensor_tensor(by_word(stats_bf[:, b, :]), woven(sum3[b]), by_word(h[3][b]), ALU.add)
        for b in range(BLOCKS):
            nc.vector.scalar_tensor_tensor(by_word(var[b]), by_word(q3[b]), 0.5, woven(q12[b]), ALU.mult, ALU.add)
        for b in range(BLOCKS):
            nc.scalar.activation(out=stats_bf[:, BLOCKS + b, :], in_=var[b][:], func=ACT.Sqrt, scale=2.0 / 3.0)
        for rows in (slice(0, BLOCKS + 1), slice(BLOCKS + 1, BLOCKS + 2), slice(BLOCKS + 2, 2 * BLOCKS)):
            nc.vector.quantize_mx(
                out=stats_codes[:, rows, :].rearrange("p r c -> p (r c)").bitcast(FP8X4),
                scales=stats_scales[:, rows, :].rearrange("p r c -> p (r c)"),
                in_=stats_bf[:, rows, :].rearrange("p r c -> p (r c)"),
            )

        for b in range(BLOCKS):
            passes = [(w2_codes, w23_scales[:, 0:N], b), (w3_codes, w23_scales[:, N : 2 * N], BLOCKS + b)]
            bank = bank_tile(b)
            for u, (codes, scales, row) in enumerate(passes):
                nc.tensor.matmul_mx(
                    out=bank[:, 0, :],
                    lhsT=codes[:].bitcast(FP8X4),
                    lhsT_scale=scales,
                    rhs=stats_codes[:, row, :].bitcast(FP8X4),
                    rhs_scale=stats_scales[:, row, :],
                    start=(u == 0),
                    stop=(u == 1),
                )
            result = keep.tile([P, P], F32, name="result%d" % b)
            nc.scalar.activation(out=result[:], in_=bank[:, 0, :], func=ACT.Copy, scale=1.0 / D)
            nc.sync.dma_start(out=out[:, b * P : (b + 1) * P], in_=result[:])
